import numpy as np
import ml_dtypes


def mxq(x, axis, fmt="e4m3"):
    dtype, down = {"e4m3": (ml_dtypes.float8_e4m3fn, 7), "e5m2": (ml_dtypes.float8_e5m2, 14)}[fmt]
    v = np.moveaxis(np.asarray(x, np.float32).astype(ml_dtypes.bfloat16).astype(np.float64), axis, -1)
    blocks = v.reshape(v.shape[:-1] + (-1, 32))
    amax = np.abs(blocks).max(-1, keepdims=True)
    byte = np.maximum(np.where(amax > 0, np.frexp(amax)[1] - 1 + 127, 0) - down, 1)
    scale = np.exp2(byte - 127.0)
    codes = (blocks / scale).astype(np.float32).astype(dtype).astype(np.float64)
    return np.moveaxis((codes * scale).reshape(v.shape), -1, axis)


WIDE = False


def mx_kscale(k):
    if not WIDE:
        return np.ones(k)
    levels = np.array([10, -10, 5, -5, 0])
    if k % 512:
        return np.exp2(np.random.permutation(np.resize(levels, k // 32))).repeat(32)
    a = np.empty((k // 512, 16))
    for p in range(k // 512):
        a[p, :8] = np.random.permutation(np.resize(levels, 8))
        for g in range(8):
            far = levels[np.abs(levels - a[p, g]) >= 10]
            a[p, g + 8] = far[np.random.randint(len(far))]
    return np.exp2(a.ravel()).repeat(32)


def f64(x):
    return np.asarray(x).astype(np.float64)


def striped(idx):
    return np.tile(idx.reshape(-1, 16).T, (8, 1)).astype(np.uint16)


def unstriped(offs):
    return offs[:16].T.reshape(-1).astype(np.int64)


def striped8(idx):
    return np.concatenate([x.reshape(-1, 16).T for x in idx]).astype(np.uint16)


def runs(offs, k):
    lists = np.stack([offs[16 * r : 16 * r + 16].T.reshape(-1) for r in range(8)]).astype(np.int64)
    return lists[np.arange(k) % 512 // 64]


def pack_weight(w):
    k, n = w.shape
    w = f64(np.asarray(w, np.float32).astype(ml_dtypes.bfloat16)).reshape(k // 32, 32, n)
    amax = np.abs(w).max(1)
    byte = np.clip(np.where(amax > 0, np.frexp(amax)[1] - 1 + 127 - 7, 1), 1, 254)
    scaled = (w * np.exp2(127.0 - byte)[:, None, :]).reshape(k, n).astype(np.float32)
    words = np.ascontiguousarray(scaled.reshape(k // 512, 128, 4, n).transpose(0, 1, 3, 2)).astype(ml_dtypes.float8_e4m3fn).view(np.uint8)
    return words, np.ascontiguousarray(byte.astype(np.uint8).reshape(k // 512, 16, n))


def unpack_weight(words, scales):
    g, p, n, _ = words.shape
    vals = np.ascontiguousarray(words).view(ml_dtypes.float8_e4m3fn).astype(np.float64) * np.repeat(np.exp2(scales.astype(np.float64) - 127.0), 8, axis=1)[..., None]
    return vals.transpose(0, 1, 3, 2).reshape(g * 512, n)


E2M1 = np.array([0.0, 0.5, 1.0, 1.5, 2.0, 3.0, 4.0, 6.0, -0.0, -0.5, -1.0, -1.5, -2.0, -3.0, -4.0, -6.0])


def pack_fp4(w):
    k, n = w.shape
    w = f64(np.asarray(w, np.float32).astype(ml_dtypes.bfloat16)).reshape(k // 32, 32, n)
    amax = np.abs(w).max(1)
    mant, ex = np.frexp(amax / 6.0)
    byte = np.clip(np.where(amax > 0, np.where(mant > 0.5, ex, ex - 1) + 127, 1), 1, 254)
    scaled = (w * np.exp2(127.0 - byte)[:, None, :]).reshape(k, n).astype(np.float32)
    c = np.ascontiguousarray(scaled.reshape(k // 512, 128, 4, n).transpose(0, 1, 3, 2)).astype(ml_dtypes.float4_e2m1fn).view(np.uint8) & 0xF
    words = (c[..., 0::2] | (c[..., 1::2] << 4)).reshape(k // 512, 128, 2 * n)
    return np.ascontiguousarray(words), np.ascontiguousarray(byte.astype(np.uint8).reshape(k // 512, 16, n))


def unpack_fp4(words, scales):
    g, _, n = scales.shape
    words = np.ascontiguousarray(words).reshape(g, 128, n, 2)
    nib = np.empty((g, 128, n, 4), np.uint8)
    nib[..., 0::2] = words & 0xF
    nib[..., 1::2] = words >> 4
    vals = E2M1[nib] * np.repeat(np.exp2(scales.astype(np.float64) - 127.0), 8, axis=1)[..., None]
    return vals.transpose(0, 1, 3, 2).reshape(g * 512, n)


def sigmoid(v):
    return 1.0 / (1.0 + np.exp(-np.maximum(v, -700.0)))

def planes(y):
    n, m = y.shape
    v = y.astype(np.float32).astype(ml_dtypes.bfloat16).astype(np.float64).reshape(n // 32, 32, m)
    top = np.abs(v).max(1)
    byte = np.clip(np.where(top > 0, np.frexp(top)[1] - 1 + 127 - 7, 1), 1, 254)
    codes = (v * np.exp2(127.0 - byte)[:, None, :]).reshape(n, m).astype(np.float32).astype(ml_dtypes.float8_e4m3fn).view(np.uint8)
    words = codes.reshape(n // 512, 128, 4, m).transpose(0, 1, 3, 2)
    return np.ascontiguousarray(words), np.ascontiguousarray(byte.astype(np.uint8).reshape(n // 512, 16, m))


K, T, S, N, H = 512, 2048, 512, 512, 512


def setup_inputs():
    n = np.random.standard_normal
    s = mx_kscale(K)[:, None]
    u = mx_kscale(H)
    packed_xT = pack_weight(n((K, T)) * s)
    packed_w1 = pack_fp4(n((K, H)) / np.sqrt(K) / s)
    packed_w2 = pack_fp4(n((H, N)) / np.sqrt(2 * H) / u[:, None])
    packed_w3 = pack_fp4(n((H, N)) / np.sqrt(2 * H) / u[:, None])
    return {
        "x_words": packed_xT[0],
        "x_scales": packed_xT[1],
        "w1_words": packed_w1[0],
        "w1_scales": packed_w1[1],
        "gn": (np.random.uniform(0.5, 1.5, (H, 1)) * u[:, None]).astype(np.float32),
        "gm": (np.random.uniform(0.5, 1.5, (H, 1)) * u[:, None]).astype(np.float32),
        "w2_words": packed_w2[0],
        "w2_scales": packed_w2[1],
        "w3_words": packed_w3[0],
        "w3_scales": packed_w3[1],
        "offs": striped(np.random.permutation(T)[:S]),
        "n1": striped8(np.stack([np.random.permutation(S) for _ in range(8)])),
        "n2": striped8(np.stack([np.random.permutation(S) for _ in range(8)])),
        "n3": striped8(np.stack([np.random.permutation(S) for _ in range(8)])),
        "n4": striped8(np.stack([np.random.permutation(S) for _ in range(8)])),
        "n5": striped8(np.stack([np.random.permutation(S) for _ in range(8)])),
    }


def reference(x_words, x_scales, w1_words, w1_scales, gn, gm, w2_words, w2_scales, w3_words, w3_scales, offs, n1, n2, n3, n4, n5):
    xq = unpack_weight(x_words, x_scales)[:, unstriped(offs)]
    y = unpack_fp4(w1_words, w1_scales).T @ xq
    ex = np.exp(y)
    z = f64(gn) * (np.log(ex + ex[np.arange(H)[:, None], runs(n1, H)]) - (y[np.arange(H)[:, None], runs(n2, H)]))
    pa = y[np.arange(H)[:, None], runs(n3, H)]
    pb = y[np.arange(H)[:, None], runs(n4, H)]
    z2 = f64(gm) * (np.maximum(np.minimum(y, pa), np.minimum(np.maximum(y, pa), pb)))
    h = unpack_fp4(w2_words, w2_scales).T @ mxq(z, 0, "e4m3") + unpack_fp4(w3_words, w3_scales).T @ mxq(z2, 0, "e4m3")
    out_0 = h * (sigmoid(h[np.arange(N)[:, None], runs(n5, N)]))
    return (out_0,) + planes(out_0)

@@ -1,0 +1,250 @@
+from contextlib import ExitStack
+
+import concourse.mybir as mybir
+
+K, T, S, N, H = 512, 2048, 512, 512, 512
+FLOPS = 3 * 2 * 512 * 512 * 512
+
+F32 = mybir.dt.float32
+BF16 = mybir.dt.bfloat16
+I32 = mybir.dt.int32
+U32 = mybir.dt.uint32
+U16 = mybir.dt.uint16
+U8 = mybir.dt.uint8
+FP8X4 = mybir.dt.float8_e4m3fn_x4
+FP4X4 = mybir.dt.float4_e2m1fn_x4
+ALU = mybir.AluOpType
+ACT = mybir.ActivationFunctionType
+
+P = 128
+PACK = 4
+HALF = S // 2
+GROUP = 128
+HALVES = [(0, HALF), (HALF, HALF)]
+Z_BLOCKS = [(0, 256), (256, 128), (384, 128)]
+
+
+def tile_picked_joinlsemedgate_none_po_kernel(
+    tc, x_words, x_scales, w1_words, w1_scales, gn, gm, w2_words, w2_scales, w3_words, w3_scales,
+    offs, n1, n2, n3, n4, n5, out_0, out_1, out_2,
+):
+    nc = tc.nc
+    with ExitStack() as ctx:
+        sb = ctx.enter_context(tc.tile_pool(name="sb", bufs=1))
+        ps = ctx.enter_context(tc.psum_pool(name="ps", bufs=1))
+
+        def new(shape, dtype, name):
+            return sb.tile(shape, dtype, name=name, align_bytes=64)
+
+        def load_list(src, name):
+            tile = sb.tile([P, S // 16], U16, name=name)
+            nc.sync.dma_start(tile[:], src)
+            return tile
+
+        def entries(lst, start, width):
+            return lst[:, start // 16 : (start + width) // 16]
+
+        def load_scale_rows(queue, tile, src, quadrants):
+            for q in quadrants:
+                queue.dma_start(tile[32 * q : 32 * q + 4, :].bitcast(I32), src[0, 4 * q : 4 * q + 4, :].bitcast(I32))
+
+        def load_words(queue, src, name):
+            raw = new([P, 2 * H], U8, name)
+            queue.dma_start(raw[:].bitcast(I32), src[0].bitcast(I32))
+            return raw
+
+        def deal_words(raw_words, name):
+            words = new([P, 2 * H], U8, name)
+            nc.vector.tensor_copy(
+                words[:].rearrange("p (t c i b) -> p c t i b", t=PACK, i=8, b=2),
+                raw_words[:].rearrange("p (c i t b) -> p c t i b", t=PACK, i=8, b=2),
+            )
+            return words
+
+        def deal_scales(raw_scales, name):
+            scales = new([P, H], U8, name)
+            nc.vector.tensor_copy(
+                scales[:].rearrange("p (t c i) -> p c t i", t=PACK, i=16),
+                raw_scales[:].rearrange("p (c i t) -> p c t i", t=PACK, i=16),
+            )
+            return scales
+
+        xw = new([P, T], I32, "xw")
+        xs = new([P, T], U8, "xs")
+        w1s_raw = new([P, H], U8, "w1s_raw")
+        w2s_raw = new([P, N], U8, "w2s_raw")
+        w3s_raw = new([P, N], U8, "w3s_raw")
+        gm_t = new([P, PACK], F32, "gm_t")
+        gn_t = new([P, PACK], F32, "gn_t")
+        nc.gpsimd.dma_start(gn_t[:], gn.rearrange("(p t) o -> p (t o)", t=PACK))
+        nc.vector.memset(w1s_raw[:].bitcast(I32), 0)
+        nc.vector.memset(xs[:].bitcast(I32), 0)
+
+        l0 = load_list(offs, "l0")
+        w1w_raw = load_words(nc.sync, w1_words, "w1w_raw")
+        nc.sync.dma_start(xw[:], x_words[0].rearrange("p n t -> p (n t)").bitcast(I32))
+        load_scale_rows(nc.gpsimd, w1s_raw, w1_scales, range(3))
+        load_scale_rows(nc.sync, w1s_raw, w1_scales, range(3, 4))
+        load_scale_rows(nc.sync, xs, x_scales, range(4))
+        nc.gpsimd.dma_start(gm_t[:], gm.rearrange("(p t) o -> p (t o)", t=PACK))
+        nc.gpsimd.memset(w3s_raw[:].bitcast(I32), 0)
+        nc.gpsimd.memset(w2s_raw[:].bitcast(I32), 0)
+        w3w_raw = load_words(nc.sync, w3_words, "w3w_raw")
+        w2w_raw = load_words(nc.sync, w2_words, "w2w_raw")
+        l3 = load_list(n3, "l3")
+        l4 = load_list(n4, "l4")
+        l1 = load_list(n1, "l1")
+        load_scale_rows(nc.sync, w3s_raw, w3_scales, range(4))
+        load_scale_rows(nc.sync, w2s_raw, w2_scales, range(4))
+        l2 = load_list(n2, "l2")
+        l5 = load_list(n5, "l5")
+
+        w1w = deal_words(w1w_raw, "w1w")
+        xgs = new([P, S], U8, "xgs")
+        xgw = new([P, S], U32, "xgw")
+        nc.vector.tensor_copy(xgs[:], xs[:].indirect(l0[:]))
+        nc.vector.tensor_copy(xgw[:], xw[:].bitcast(U32).indirect(l0[:]))
+        w1s = deal_scales(w1s_raw, "w1s")
+        w3w = deal_words(w3w_raw, "w3w")
+        w2w = deal_words(w2w_raw, "w2w")
+
+        def weights(words, scales, t):
+            return dict(
+                lhsT=words[:, 2 * P * t : 2 * P * (t + 1)].bitcast(FP4X4),
+                lhsT_scale=scales[:, P * t : P * (t + 1)],
+            )
+
+        y_ps = []
+        for t in range(PACK):
+            bank = ps.tile([P, S], F32, name="y_ps%d" % t, tag="bank%d" % t)
+            nc.tensor.matmul_mx(out=bank[:], rhs=xgw[:].bitcast(FP8X4), rhs_scale=xgs[:], start=True, stop=True, **weights(w1w, w1s, t))
+            y_ps.append(bank)
+
+        neg_gn = new([P, PACK], F32, "neg_gn")
+        nc.scalar.activation(neg_gn[:], gn_t[:], ACT.Copy, scale=-1.0)
+
+        ym = [new([P, S], F32, "ym%d" % t) for t in range(PACK)]
+        y = [new([P, S], F32, "y%d" % t) for t in range(PACK)]
+        ymb = new([P, PACK, S], BF16, "ymb")
+        ex = new([P, PACK, S], F32, "ex")
+        for t in range(PACK):
+            nc.scalar.activation(ym[t][:], y_ps[t][:], ACT.Copy, scale=gm_t[:, t : t + 1])
+        for t in range(PACK):
+            nc.scalar.activation(ymb[:, t, :], y_ps[t][:], ACT.Copy, scale=gm_t[:, t : t + 1])
+        for t in range(PACK):
+            nc.scalar.copy(y[t][:], y_ps[t][:])
+        for t in range(PACK):
+            nc.scalar.activation(ex[:, t, :], y_ps[t][:], ACT.Exp)
+        ex1 = [new([P, PACK, HALF], F32, "ex1_%d" % a) for a in range(2)]
+        for a, (c0, w) in enumerate(HALVES):
+            for t in range(PACK):
+                nc.scalar.activation(ex1[a][:, t, :], y[t][:].indirect(entries(l1, c0, w)), ACT.Exp)
+
+        pa = [new([P, PACK, HALF], BF16, "pa%d" % a) for a in range(2)]
+        pb = [new([P, PACK, HALF], BF16, "pb%d" % a) for a in range(2)]
+        for t in range(PACK):
+            for a, (c0, w) in enumerate(HALVES):
+                nc.vector.tensor_copy(pa[a][:, t, :], ym[t][:].indirect(entries(l3, c0, w)))
+                nc.vector.tensor_copy(pb[a][:, t, :], ym[t][:].indirect(entries(l4, c0, w)))
+        w3s = deal_scales(w3s_raw, "w3s")
+        w2s = deal_scales(w2s_raw, "w2s")
+        lo = [new([P, PACK, HALF], BF16, "lo%d" % a) for a in range(2)]
+        hi = [new([P, PACK, HALF], BF16, "hi%d" % a) for a in range(2)]
+        mid = [new([P, PACK, HALF], BF16, "mid%d" % a) for a in range(2)]
+        med = [new([P, PACK, HALF], BF16, "med%d" % a) for a in range(2)]
+        for a, (c0, w) in enumerate(HALVES):
+            nc.vector.tensor_tensor(hi[a][:], ymb[:, :, c0 : c0 + w], pa[a][:], ALU.max)
+            nc.vector.tensor_tensor(lo[a][:], ymb[:, :, c0 : c0 + w], pa[a][:], ALU.min)
+        for a in range(2):
+            nc.vector.tensor_tensor(mid[a][:], hi[a][:], pb[a][:], ALU.min)
+
+        sm = [new([P, PACK, HALF], F32, "sm%d" % a) for a in range(2)]
+        lg = [new([P, PACK, HALF], F32, "lg%d" % a) for a in range(2)]
+        for a, (c0, w) in enumerate(HALVES):
+            nc.vector.tensor_tensor(sm[a][:], ex[:, :, c0 : c0 + w], ex1[a][:], ALU.add)
+        for a in range(2):
+            nc.vector.tensor_tensor(med[a][:], lo[a][:], mid[a][:], ALU.max)
+        for a in range(2):
+            nc.scalar.activation(lg[a][:], sm[a][:], ACT.Ln)
+
+        def quantise(src, width, name):
+            codes = new([P, width], U32, name + "_codes")
+            scales = new([P, width], U8, name + "_scales")
+            nc.vector.quantize_mx(out=codes[:].bitcast(FP8X4), scales=scales[:], in_=src[:])
+            return codes, scales
+
+        def woven(tile, i):
+            return tile[:].rearrange("p (c i t) -> p c t i", t=PACK, i=i)
+
+        def planar(view, i):
+            return view.rearrange("p t (c i) -> p c t i", i=i)
+
+        z2q = []
+        for a in range(2):
+            z2b = new([P, HALF * PACK], BF16, "z2b%d" % a)
+            nc.scalar.copy(woven(z2b, 4), planar(med[a][:], 4))
+            z2q.append(quantise(z2b, HALF, "z2q%d" % a))
+
+        h_ps = [[None] * PACK, [None] * PACK]
+        for t in range(PACK):
+            h_ps[0][t] = ps.tile([P, S], F32, name="h_ps0_%d" % t, tag="bank%d" % (PACK + t))
+            h_ps[1][t] = ps.tile([P, S], F32, name="h_ps1_%d" % t, tag="bank%d" % t)
+        h = [new([P, S], F32, "h%d" % t) for t in range(PACK)]
+        sg0 = new([P, S], F32, "sg0")
+        for b, (c0, w) in enumerate(Z_BLOCKS):
+            a, ca = divmod(c0, HALF)
+            last = b == len(Z_BLOCKS) - 1
+            banks = h_ps[1 if last else 0]
+            v = new([P, PACK, w], F32, "v%d" % b)
+            for t in range(PACK):
+                nc.vector.tensor_tensor(v[:, t, :], y[t][:].indirect(entries(l2, c0, w)), lg[a][:, t, ca : ca + w], ALU.subtract)
+            zb = new([P, w * PACK], BF16, "zb%d" % b)
+            gain = neg_gn[:].unsqueeze(1).unsqueeze(3).to_broadcast([P, w // 2, PACK, 2])
+            nc.vector.tensor_tensor(woven(zb, 2), planar(v[:], 2), gain, ALU.mult)
+            zc, zs = quantise(zb, w, "zq%d" % b)
+            for g in range(0, w, GROUP):
+                cols = slice(c0 + g, c0 + g + GROUP)
+                for t in range(PACK):
+                    z2c, z2s = z2q[a]
+                    z2_cols = slice(ca + g, ca + g + GROUP)
+                    nc.tensor.matmul_mx(out=banks[t][:, cols], rhs=z2c[:, z2_cols].bitcast(FP8X4), rhs_scale=z2s[:, z2_cols],
+                                        start=True, stop=False, **weights(w3w, w3s, t))
+                for t in range(PACK):
+                    nc.tensor.matmul_mx(out=banks[t][:, cols], rhs=zc[:, g : g + GROUP].bitcast(FP8X4), rhs_scale=zs[:, g : g + GROUP],
+                                        start=False, stop=True, **weights(w2w, w2s, t))
+            cols = slice(c0, c0 + w)
+            for t in range(PACK):
+                if last and t % 2 == 0:
+                    nc.vector.tensor_copy(h[t][:, cols], banks[t][:, cols])
+                else:
+                    nc.scalar.copy(h[t][:, cols], banks[t][:, cols])
+            nc.scalar.activation(sg0[:, cols], banks[0][:, cols], ACT.Sigmoid)
+
+        out_rows = out_0.rearrange("(p t) c -> p t c", t=PACK)
+        out_words = out_1[0].rearrange("p n t -> p (n t)").bitcast(I32)
+        oc = new([P, S], U32, "oc")
+        osc = new([P, S], U8, "osc")
+        o = [new([P, PACK, w], F32, "o%d" % a) for a, (c0, w) in enumerate(Z_BLOCKS)]
+        sg = [new([P, PACK, w], F32, "sg_%d" % a) for a, (c0, w) in enumerate(Z_BLOCKS)]
+        ob = [new([P, w * PACK], BF16, "ob%d" % a) for a, (c0, w) in enumerate(Z_BLOCKS)]
+        for a, (c0, w) in enumerate(Z_BLOCKS):
+            for t in range(1, PACK):
+                nc.scalar.activation(sg[a][:, t, :], h[t][:].indirect(entries(l5, c0, w)), ACT.Sigmoid)
+        for a, (c0, w) in enumerate(Z_BLOCKS):
+            nc.vector.tensor_tensor(o[a][:, 0, :], sg0[:].indirect(entries(l5, c0, w)), h[0][:, c0 : c0 + w], ALU.mult)
+
+        def planes(a):
+            c0, w = Z_BLOCKS[a]
+            nc.vector.quantize_mx(out=oc[:, c0 : c0 + w].bitcast(FP8X4), scales=osc[:, c0 : c0 + w], in_=ob[a][:])
+            nc.sync.dma_start(out_words[:, c0 : c0 + w], oc[:, c0 : c0 + w].bitcast(I32))
+
+        for a, (c0, w) in enumerate(Z_BLOCKS):
+            for t in range(1, PACK):
+                nc.vector.tensor_tensor(o[a][:, t, :], sg[a][:, t, :], h[t][:, c0 : c0 + w], ALU.mult)
+            nc.sync.dma_start(out_rows[:, :, c0 : c0 + w], o[a][:])
+            if a > 0:
+                planes(a - 1)
+            nc.vector.tensor_copy(woven(ob[a], 4), planar(o[a][:], 4))
+        planes(len(Z_BLOCKS) - 1)
+        for q in range(4):
+            nc.scalar.dma_start(out_2[0, 4 * q : 4 * q + 4, :].bitcast(I32), osc[32 * q : 32 * q + 4, :].bitcast(I32))

@@ -76,27 +76,27 @@ def tile_picked_joinlsemedgate_none_po_kernel(
         w3s_raw = new([P, N], U8, "w3s_raw")
         gm_t = new([P, PACK], F32, "gm_t")
         gn_t = new([P, PACK], F32, "gn_t")
-        nc.gpsimd.dma_start(gn_t[:], gn.rearrange("(p t) o -> p (t o)", t=PACK))
-        nc.vector.memset(w1s_raw[:].bitcast(I32), 0)
-        nc.vector.memset(xs[:].bitcast(I32), 0)
+        nc.gpsimd.memset(xs[:].bitcast(I32), 0)
+        nc.gpsimd.memset(w1s_raw[:].bitcast(I32), 0)
+        nc.vector.memset(w3s_raw[:].bitcast(I32), 0)
+        nc.vector.memset(w2s_raw[:].bitcast(I32), 0)
 
         l0 = load_list(offs, "l0")
         w1w_raw = load_words(nc.sync, w1_words, "w1w_raw")
-        nc.sync.dma_start(xw[:], x_words[0].rearrange("p n t -> p (n t)").bitcast(I32))
-        load_scale_rows(nc.gpsimd, w1s_raw, w1_scales, range(3))
-        load_scale_rows(nc.sync, w1s_raw, w1_scales, range(3, 4))
+        nc.sync.dma_start(gn_t[:], gn.rearrange("(p t) o -> p (t o)", t=PACK))
         load_scale_rows(nc.sync, xs, x_scales, range(4))
-        nc.gpsimd.dma_start(gm_t[:], gm.rearrange("(p t) o -> p (t o)", t=PACK))
-        nc.gpsimd.memset(w3s_raw[:].bitcast(I32), 0)
-        nc.gpsimd.memset(w2s_raw[:].bitcast(I32), 0)
-        w3w_raw = load_words(nc.sync, w3_words, "w3w_raw")
-        w2w_raw = load_words(nc.sync, w2_words, "w2w_raw")
+        nc.sync.dma_start(xw[:], x_words[0].rearrange("p n t -> p (n t)").bitcast(I32))
+        load_scale_rows(nc.gpsimd, w1s_raw, w1_scales, range(1))
+        load_scale_rows(nc.sync, w1s_raw, w1_scales, range(1, 4))
+        nc.sync.dma_start(gm_t[:], gm.rearrange("(p t) o -> p (t o)", t=PACK))
         l3 = load_list(n3, "l3")
         l4 = load_list(n4, "l4")
+        w3w_raw = load_words(nc.sync, w3_words, "w3w_raw")
+        w2w_raw = load_words(nc.sync, w2_words, "w2w_raw")
         l1 = load_list(n1, "l1")
+        l2 = load_list(n2, "l2")
         load_scale_rows(nc.sync, w3s_raw, w3_scales, range(4))
         load_scale_rows(nc.sync, w2s_raw, w2_scales, range(4))
-        l2 = load_list(n2, "l2")
         l5 = load_list(n5, "l5")
 
         w1w = deal_words(w1w_raw, "w1w")
@@ -130,9 +130,12 @@ def tile_picked_joinlsemedgate_none_po_kernel(
         for t in range(PACK):
             nc.scalar.activation(ym[t][:], y_ps[t][:], ACT.Copy, scale=gm_t[:, t : t + 1])
         for t in range(PACK):
-            nc.scalar.activation(ymb[:, t, :], y_ps[t][:], ACT.Copy, scale=gm_t[:, t : t + 1])
-        for t in range(PACK):
             nc.scalar.copy(y[t][:], y_ps[t][:])
+        yn = [sb.tile([P, S], F32, name="yn%d" % t, tag="yn%d" % t, align_bytes=64) for t in range(PACK)]
+        for t in range(PACK):
+            nc.gpsimd.tensor_scalar(ymb[:, t, :], ym[t][:], 1.0, 0.0, ALU.mult, ALU.add)
+        for t in range(PACK):
+            nc.gpsimd.tensor_scalar(yn[t][:], y[t][:], neg_gn[:, t : t + 1], 0.0, ALU.mult, ALU.add)
         for t in range(PACK):
             nc.scalar.activation(ex[:, t, :], y_ps[t][:], ACT.Exp)
         ex1 = [new([P, PACK, HALF], F32, "ex1_%d" % a) for a in range(2)]
@@ -148,30 +151,34 @@ def tile_picked_joinlsemedgate_none_po_kernel(
                 nc.vector.tensor_copy(pb[a][:, t, :], ym[t][:].indirect(entries(l4, c0, w)))
         w3s = deal_scales(w3s_raw, "w3s")
         w2s = deal_scales(w2s_raw, "w2s")
-        lo = [new([P, PACK, HALF], BF16, "lo%d" % a) for a in range(2)]
-        hi = [new([P, PACK, HALF], BF16, "hi%d" % a) for a in range(2)]
+        y2 = [new([P, PACK, HALF], F32, "y2_%d" % a) for a in range(2)]
+        for t in range(PACK):
+            for a, (c0, w) in enumerate(HALVES):
+                nc.vector.tensor_copy(y2[a][:, t, :], yn[t][:].indirect(entries(l2, c0, w)))
+        hi = [sb.tile([P, PACK, HALF], BF16, name="hi0", tag="yn3", align_bytes=64), None]
+        lo = [sb.tile([P, PACK, HALF], BF16, name="lo0", tag="yn2", align_bytes=64), None]
         mid = [new([P, PACK, HALF], BF16, "mid%d" % a) for a in range(2)]
-        med = [new([P, PACK, HALF], BF16, "med%d" % a) for a in range(2)]
-        for a, (c0, w) in enumerate(HALVES):
+        med = new([P, PACK, HALF], BF16, "med")
+
+        def median_bounds(a):
+            c0, w = HALVES[a]
             nc.vector.tensor_tensor(hi[a][:], ymb[:, :, c0 : c0 + w], pa[a][:], ALU.max)
             nc.vector.tensor_tensor(lo[a][:], ymb[:, :, c0 : c0 + w], pa[a][:], ALU.min)
-        for a in range(2):
             nc.vector.tensor_tensor(mid[a][:], hi[a][:], pb[a][:], ALU.min)
 
+        median_bounds(0)
+        nc.vector.tensor_tensor(med[:], lo[0][:], mid[0][:], ALU.max)
+
         sm = [new([P, PACK, HALF], F32, "sm%d" % a) for a in range(2)]
-        lg = [new([P, PACK, HALF], F32, "lg%d" % a) for a in range(2)]
+        lg = [sb.tile([P, PACK, HALF], F32, name="lg%d" % a, tag="lg%d" % a, align_bytes=64) for a in range(2)]
         for a, (c0, w) in enumerate(HALVES):
-            nc.vector.tensor_tensor(sm[a][:], ex[:, :, c0 : c0 + w], ex1[a][:], ALU.add)
-        for a in range(2):
-            nc.vector.tensor_tensor(med[a][:], lo[a][:], mid[a][:], ALU.max)
+            nc.gpsimd.tensor_tensor(sm[a][:], ex[:, :, c0 : c0 + w], ex1[a][:], ALU.add)
         for a in range(2):
             nc.scalar.activation(lg[a][:], sm[a][:], ACT.Ln)
-
-        def quantise(src, width, name):
-            codes = new([P, width], U32, name + "_codes")
-            scales = new([P, width], U8, name + "_scales")
-            nc.vector.quantize_mx(out=codes[:].bitcast(FP8X4), scales=scales[:], in_=src[:])
-            return codes, scales
+        lgn = [sb.tile([P, PACK, HALF], F32, name="lgn%d" % a, tag="lgn%d" % a, align_bytes=64) for a in range(2)]
+        for a in range(2):
+            for t in range(PACK):
+                nc.scalar.activation(lgn[a][:, t, :], lg[a][:, t, :], ACT.Copy, scale=gn_t[:, t : t + 1])
 
         def woven(tile, i):
             return tile[:].rearrange("p (c i t) -> p c t i", t=PACK, i=i)
@@ -179,46 +186,55 @@ def tile_picked_joinlsemedgate_none_po_kernel(
         def planar(view, i):
             return view.rearrange("p t (c i) -> p c t i", i=i)
 
-        z2q = []
-        for a in range(2):
-            z2b = new([P, HALF * PACK], BF16, "z2b%d" % a)
-            nc.scalar.copy(woven(z2b, 4), planar(med[a][:], 4))
-            z2q.append(quantise(z2b, HALF, "z2q%d" % a))
+        z2b = [sb.tile([P, HALF * PACK], BF16, name="z2b%d" % a, tag="lg%d" % (1 - a), align_bytes=64) for a in range(2)]
+        nc.scalar.copy(woven(z2b[0], 4), planar(med[:], 4))
 
-        h_ps = [[None] * PACK, [None] * PACK]
-        for t in range(PACK):
-            h_ps[0][t] = ps.tile([P, S], F32, name="h_ps0_%d" % t, tag="bank%d" % (PACK + t))
-            h_ps[1][t] = ps.tile([P, S], F32, name="h_ps1_%d" % t, tag="bank%d" % t)
+        zb = new([P, S * PACK], BF16, "zb")
+        for a, (c0, w) in enumerate(HALVES):
+            nc.vector.tensor_tensor(
+                zb[:, PACK * c0 : PACK * (c0 + w)].rearrange("p (c i t) -> p c t i", t=PACK, i=2),
+                planar(lgn[a][:], 2), planar(y2[a][:], 2), ALU.add)
+        hi[1] = sb.tile([P, PACK, HALF], BF16, name="hi1", tag="lgn1", align_bytes=64)
+        lo[1] = sb.tile([P, PACK, HALF], BF16, name="lo1", tag="lgn0", align_bytes=64)
+        zc = new([P, S], U32, "zc")
+        zs = new([P, S], U8, "zs")
+        z2c = new([P, S], U32, "z2c")
+        z2s = new([P, S], U8, "z2s")
+        nc.vector.quantize_mx(out=z2c[:, 0:HALF].bitcast(FP8X4), scales=z2s[:, 0:HALF], in_=z2b[0][:])
+        nc.vector.quantize_mx(out=zc[:].bitcast(FP8X4), scales=zs[:], in_=zb[:])
+        median_bounds(1)
+        for g in range(0, HALF, GROUP):
+            nc.vector.tensor_tensor(
+                z2b[1][:, PACK * g : PACK * (g + GROUP)].rearrange("p (c i t) -> p c t i", t=PACK, i=4),
+                planar(lo[1][:, :, g : g + GROUP], 4), planar(mid[1][:, :, g : g + GROUP], 4), ALU.max)
+        for g in range(0, HALF, GROUP):
+            cols = slice(HALF + g, HALF + g + GROUP)
+            nc.vector.quantize_mx(out=z2c[:, cols].bitcast(FP8X4), scales=z2s[:, cols], in_=z2b[1][:, PACK * g : PACK * (g + GROUP)])
+
         h = [new([P, S], F32, "h%d" % t) for t in range(PACK)]
         sg0 = new([P, S], F32, "sg0")
-        for b, (c0, w) in enumerate(Z_BLOCKS):
-            a, ca = divmod(c0, HALF)
-            last = b == len(Z_BLOCKS) - 1
-            banks = h_ps[1 if last else 0]
-            v = new([P, PACK, w], F32, "v%d" % b)
-            for t in range(PACK):
-                nc.vector.tensor_tensor(v[:, t, :], y[t][:].indirect(entries(l2, c0, w)), lg[a][:, t, ca : ca + w], ALU.subtract)
-            zb = new([P, w * PACK], BF16, "zb%d" % b)
-            gain = neg_gn[:].unsqueeze(1).unsqueeze(3).to_broadcast([P, w // 2, PACK, 2])
-            nc.vector.tensor_tensor(woven(zb, 2), planar(v[:], 2), gain, ALU.mult)
-            zc, zs = quantise(zb, w, "zq%d" % b)
-            for g in range(0, w, GROUP):
-                cols = slice(c0 + g, c0 + g + GROUP)
+
+        def z_pass(bank, t, c):
+            nc.tensor.matmul_mx(out=bank[:, c % HALF : c % HALF + GROUP], rhs=zc[:, c : c + GROUP].bitcast(FP8X4), rhs_scale=zs[:, c : c + GROUP],
+                                start=True, stop=False, **weights(w2w, w2s, t))
+
+        def z2_pass(bank, t, c):
+            nc.tensor.matmul_mx(out=bank[:, c % HALF : c % HALF + GROUP], rhs=z2c[:, c : c + GROUP].bitcast(FP8X4), rhs_scale=z2s[:, c : c + GROUP],
+                                start=False, stop=True, **weights(w3w, w3s, t))
+
+        for a, (c0, w) in enumerate(HALVES):
+            banks = [ps.tile([P, HALF], F32, name="h_ps%d_%d" % (a, t), tag="bank%d" % (PACK * (1 - a) + t)) for t in range(PACK)]
+            for c in range(c0, c0 + w, GROUP):
                 for t in range(PACK):
-                    z2c, z2s = z2q[a]
-                    z2_cols = slice(ca + g, ca + g + GROUP)
-                    nc.tensor.matmul_mx(out=banks[t][:, cols], rhs=z2c[:, z2_cols].bitcast(FP8X4), rhs_scale=z2s[:, z2_cols],
-                                        start=True, stop=False, **weights(w3w, w3s, t))
+                    z_pass(banks[t], t, c)
                 for t in range(PACK):
-                    nc.tensor.matmul_mx(out=banks[t][:, cols], rhs=zc[:, g : g + GROUP].bitcast(FP8X4), rhs_scale=zs[:, g : g + GROUP],
-                                        start=False, stop=True, **weights(w2w, w2s, t))
-            cols = slice(c0, c0 + w)
-            for t in range(PACK):
-                if last and t % 2 == 0:
-                    nc.vector.tensor_copy(h[t][:, cols], banks[t][:, cols])
+                    z2_pass(banks[t], t, c)
+            nc.scalar.activation(sg0[:, c0 : c0 + w], banks[0][:], ACT.Sigmoid)
+            for t in (1, 2, 3, 0) if a == 1 else range(PACK):
+                if a == 0:
+                    nc.scalar.copy(h[t][:, c0 : c0 + w], banks[t][:])
                 else:
-                    nc.scalar.copy(h[t][:, cols], banks[t][:, cols])
-            nc.scalar.activation(sg0[:, cols], banks[0][:, cols], ACT.Sigmoid)
+                    nc.vector.tensor_copy(h[t][:, c0 : c0 + w], banks[t][:])
 
         out_rows = out_0.rearrange("(p t) c -> p t c", t=PACK)
         out_words = out_1[0].rearrange("p n t -> p (n t)").bitcast(I32)
@@ -228,10 +244,9 @@ def tile_picked_joinlsemedgate_none_po_kernel(
         sg = [new([P, PACK, w], F32, "sg_%d" % a) for a, (c0, w) in enumerate(Z_BLOCKS)]
         ob = [new([P, w * PACK], BF16, "ob%d" % a) for a, (c0, w) in enumerate(Z_BLOCKS)]
         for a, (c0, w) in enumerate(Z_BLOCKS):
-            for t in range(1, PACK):
+            for t in range(1 if a == 0 else 0, PACK):
                 nc.scalar.activation(sg[a][:, t, :], h[t][:].indirect(entries(l5, c0, w)), ACT.Sigmoid)
-        for a, (c0, w) in enumerate(Z_BLOCKS):
-            nc.vector.tensor_tensor(o[a][:, 0, :], sg0[:].indirect(entries(l5, c0, w)), h[0][:, c0 : c0 + w], ALU.mult)
+        nc.vector.tensor_tensor(o[0][:, 0, :], sg0[:].indirect(entries(l5, 0, HALF)), h[0][:, 0:HALF], ALU.mult)
 
         def planes(a):
             c0, w = Z_BLOCKS[a]
@@ -239,7 +254,7 @@ def tile_picked_joinlsemedgate_none_po_kernel(
             nc.sync.dma_start(out_words[:, c0 : c0 + w], oc[:, c0 : c0 + w].bitcast(I32))
 
         for a, (c0, w) in enumerate(Z_BLOCKS):
-            for t in range(1, PACK):
+            for t in range(1 if a == 0 else 0, PACK):
                 nc.vector.tensor_tensor(o[a][:, t, :], sg[a][:, t, :], h[t][:, c0 : c0 + w], ALU.mult)
             nc.sync.dma_start(out_rows[:, :, c0 : c0 + w], o[a][:])
             if a > 0:

@@ -2,8 +2,10 @@ from contextlib import ExitStack
 
 import concourse.mybir as mybir
 
-K, T, S, N, H = 512, 2048, 512, 512, 512
-FLOPS = 3 * 2 * 512 * 512 * 512
+T = 2048
+S = 512
+C = 512
+FLOPS = 3 * 2 * 512 * C * S
 
 F32 = mybir.dt.float32
 BF16 = mybir.dt.bfloat16
@@ -18,10 +20,13 @@ ACT = mybir.ActivationFunctionType
 
 P = 128
 PACK = 4
+BANKS = 8
+LIST_ROWS = 16
+QUADRANT = 32
 HALF = S // 2
 GROUP = 128
 HALVES = [(0, HALF), (HALF, HALF)]
-Z_BLOCKS = [(0, 256), (256, 128), (384, 128)]
+BLOCKS = [(0, HALF), (HALF, GROUP), (HALF + GROUP, GROUP)]
 
 
 def tile_picked_joinlsemedgate_none_po_kernel(
@@ -33,233 +38,280 @@ def tile_picked_joinlsemedgate_none_po_kernel(
         sb = ctx.enter_context(tc.tile_pool(name="sb", bufs=1))
         ps = ctx.enter_context(tc.psum_pool(name="ps", bufs=1))
 
-        def new(shape, dtype, name):
-            return sb.tile(shape, dtype, name=name, align_bytes=64)
+        def new(shape, dtype, name, tag=None):
+            return sb.tile(shape, dtype, name=name, tag=tag or name, align_bytes=64)
 
         def load_list(src, name):
-            tile = sb.tile([P, S // 16], U16, name=name)
+            tile = sb.tile([P, S // LIST_ROWS], U16, name=name)
             nc.sync.dma_start(tile[:], src)
             return tile
 
-        def entries(lst, start, width):
-            return lst[:, start // 16 : (start + width) // 16]
+        def entries(lst, c0, w):
+            return lst[:, c0 // LIST_ROWS : (c0 + w) // LIST_ROWS]
 
-        def load_scale_rows(queue, tile, src, quadrants):
-            for q in quadrants:
-                queue.dma_start(tile[32 * q : 32 * q + 4, :].bitcast(I32), src[0, 4 * q : 4 * q + 4, :].bitcast(I32))
+        def scale_rows(tile, q):
+            return tile[QUADRANT * q : QUADRANT * q + PACK, :].bitcast(I32)
 
-        def load_words(queue, src, name):
-            raw = new([P, 2 * H], U8, name)
-            queue.dma_start(raw[:].bitcast(I32), src[0].bitcast(I32))
+        def load_scales(tile, src):
+            for q in range(P // QUADRANT):
+                nc.sync.dma_start(scale_rows(tile, q), src[0, PACK * q : PACK * (q + 1), :].bitcast(I32))
+
+        def load_words(src, name):
+            raw = new([P, 2 * C], U8, name)
+            nc.sync.dma_start(raw[:].bitcast(I32), src[0].bitcast(I32))
             return raw
 
-        def deal_words(raw_words, name):
-            words = new([P, 2 * H], U8, name)
+        def load_gain(queue, tile, src):
+            queue.dma_start(tile[:], src.rearrange("(p t) o -> p (t o)", t=PACK))
+
+        def deal_words(raw, name):
+            words = new([P, 2 * C], U8, name)
             nc.vector.tensor_copy(
                 words[:].rearrange("p (t c i b) -> p c t i b", t=PACK, i=8, b=2),
-                raw_words[:].rearrange("p (c i t b) -> p c t i b", t=PACK, i=8, b=2),
+                raw[:].rearrange("p (c i t b) -> p c t i b", t=PACK, i=8, b=2),
             )
             return words
 
-        def deal_scales(raw_scales, name):
-            scales = new([P, H], U8, name)
-            nc.vector.tensor_copy(
-                scales[:].rearrange("p (t c i) -> p c t i", t=PACK, i=16),
-                raw_scales[:].rearrange("p (c i t) -> p c t i", t=PACK, i=16),
-            )
-            return scales
+        def dealt_bytes(tile):
+            return tile[:].rearrange("p (t c i) -> p c t i", t=PACK, i=16)
 
-        xw = new([P, T], I32, "xw")
-        xs = new([P, T], U8, "xs")
-        w1s_raw = new([P, H], U8, "w1s_raw")
-        w2s_raw = new([P, N], U8, "w2s_raw")
-        w3s_raw = new([P, N], U8, "w3s_raw")
+        def raw_bytes(tile):
+            return tile[:].rearrange("p (c i t) -> p c t i", t=PACK, i=16)
+
+        def woven(view, run):
+            return view.rearrange("p (c i t) -> p c t i", t=PACK, i=run)
+
+        def planar(view, run):
+            return view.rearrange("p t (c i) -> p c t i", i=run)
+
+        x_w = new([P, T], I32, "x_w")
+        x_s = new([P, T], U8, "x_s")
+        w1_s_raw = new([P, C], U8, "w1_s_raw")
+        w2_s_raw = new([P, C], U8, "w2_s_raw")
+        w3_s_raw = new([P, C], U8, "w3_s_raw")
         gm_t = new([P, PACK], F32, "gm_t")
         gn_t = new([P, PACK], F32, "gn_t")
-        nc.gpsimd.memset(xs[:].bitcast(I32), 0)
-        nc.gpsimd.memset(w1s_raw[:].bitcast(I32), 0)
-        nc.vector.memset(w3s_raw[:].bitcast(I32), 0)
-        nc.vector.memset(w2s_raw[:].bitcast(I32), 0)
+        nc.gpsimd.memset(x_s[:].bitcast(I32), 0)
+        for raw in (w1_s_raw, w3_s_raw, w2_s_raw):
+            nc.vector.memset(raw[:].bitcast(I32), 0)
 
-        l0 = load_list(offs, "l0")
-        w1w_raw = load_words(nc.sync, w1_words, "w1w_raw")
-        nc.sync.dma_start(gn_t[:], gn.rearrange("(p t) o -> p (t o)", t=PACK))
-        load_scale_rows(nc.sync, xs, x_scales, range(4))
-        nc.sync.dma_start(xw[:], x_words[0].rearrange("p n t -> p (n t)").bitcast(I32))
-        load_scale_rows(nc.gpsimd, w1s_raw, w1_scales, range(1))
-        load_scale_rows(nc.sync, w1s_raw, w1_scales, range(1, 4))
-        nc.sync.dma_start(gm_t[:], gm.rearrange("(p t) o -> p (t o)", t=PACK))
-        l3 = load_list(n3, "l3")
-        l4 = load_list(n4, "l4")
-        w3w_raw = load_words(nc.sync, w3_words, "w3w_raw")
-        w2w_raw = load_words(nc.sync, w2_words, "w2w_raw")
-        l1 = load_list(n1, "l1")
-        l2 = load_list(n2, "l2")
-        load_scale_rows(nc.sync, w3s_raw, w3_scales, range(4))
-        load_scale_rows(nc.sync, w2s_raw, w2_scales, range(4))
-        l5 = load_list(n5, "l5")
+        picks = load_list(offs, "picks")
+        w1_w_raw = load_words(w1_words, "w1_w_raw")
+        w3_w_raw = load_words(w3_words, "w3_w_raw")
+        load_scales(x_s, x_scales)
+        nc.sync.dma_start(x_w[:], x_words[0].rearrange("p n t -> p (n t)").bitcast(I32))
+        load_gain(nc.gpsimd, gm_t, gm)
+        load_scales(w1_s_raw, w1_scales)
+        w2_w_raw = load_words(w2_words, "w2_w_raw")
+        load_gain(nc.sync, gn_t, gn)
+        list3 = load_list(n3, "list3")
+        list4 = load_list(n4, "list4")
+        list1 = load_list(n1, "list1")
+        load_scales(w3_s_raw, w3_scales)
+        load_scales(w2_s_raw, w2_scales)
+        list2 = load_list(n2, "list2")
+        list5 = load_list(n5, "list5")
 
-        w1w = deal_words(w1w_raw, "w1w")
-        xgs = new([P, S], U8, "xgs")
-        xgw = new([P, S], U32, "xgw")
-        nc.vector.tensor_copy(xgs[:], xs[:].indirect(l0[:]))
-        nc.vector.tensor_copy(xgw[:], xw[:].bitcast(U32).indirect(l0[:]))
-        w1s = deal_scales(w1s_raw, "w1s")
-        w3w = deal_words(w3w_raw, "w3w")
-        w2w = deal_words(w2w_raw, "w2w")
+        w1_w = deal_words(w1_w_raw, "w1_w")
+        picked_s = new([P, S], U8, "picked_s")
+        picked_w = new([P, S], U32, "picked_w")
+        nc.vector.tensor_copy(picked_s[:], x_s[:].indirect(picks[:]))
+        w3_w = deal_words(w3_w_raw, "w3_w")
+        w1_s = new([P, C], U8, "w1_s")
+        nc.vector.tensor_copy(w1_s[:, :P], w1_s_raw[:, ::PACK])
+        nc.vector.tensor_copy(dealt_bytes(w1_s)[:, :, 1:, :], raw_bytes(w1_s_raw)[:, :, 1:, :])
+        for c0, w in HALVES:
+            nc.vector.tensor_copy(picked_w[:, c0 : c0 + w], x_w[:].bitcast(U32).indirect(entries(picks, c0, w)))
+        w2_w = deal_words(w2_w_raw, "w2_w")
 
-        def weights(words, scales, t):
-            return dict(
+        def product(bank, words, scales, t, codes, code_scales, start, stop):
+            nc.tensor.matmul_mx(
+                out=bank,
                 lhsT=words[:, 2 * P * t : 2 * P * (t + 1)].bitcast(FP4X4),
                 lhsT_scale=scales[:, P * t : P * (t + 1)],
+                rhs=codes.bitcast(FP8X4),
+                rhs_scale=code_scales,
+                start=start,
+                stop=stop,
             )
 
-        y_ps = []
-        for t in range(PACK):
-            bank = ps.tile([P, S], F32, name="y_ps%d" % t, tag="bank%d" % t)
-            nc.tensor.matmul_mx(out=bank[:], rhs=xgw[:].bitcast(FP8X4), rhs_scale=xgs[:], start=True, stop=True, **weights(w1w, w1s, t))
-            y_ps.append(bank)
+        pieces = [(0, c0, w) for c0, w in HALVES] + [(t, 0, S) for t in range(1, PACK)]
+        y_banks = []
+        for n, (t, c0, w) in enumerate(pieces):
+            bank = ps.tile([P, w], F32, name="y_bank%d" % n, tag="bank%d" % ((n - 1) % BANKS))
+            product(bank[:], w1_w, w1_s, t, picked_w[:, c0 : c0 + w], picked_s[:, c0 : c0 + w], True, True)
+            y_banks.append((bank, t, slice(c0, c0 + w)))
 
-        neg_gn = new([P, PACK], F32, "neg_gn")
-        nc.scalar.activation(neg_gn[:], gn_t[:], ACT.Copy, scale=-1.0)
-
-        ym = [new([P, S], F32, "ym%d" % t) for t in range(PACK)]
+        ym = [new([P, 2 * S], F32, "ym%d" % t) for t in range(PACK)]
+        yn_ex = [new([P, 2 * S], F32, "yn_ex%d" % t) for t in range(PACK)]
         y = [new([P, S], F32, "y%d" % t) for t in range(PACK)]
-        ymb = new([P, PACK, S], BF16, "ymb")
-        ex = new([P, PACK, S], F32, "ex")
+        zero = new([P, 1], F32, "zero")
+        nc.vector.memset(zero[:], 0.0)
         for t in range(PACK):
-            nc.scalar.activation(ym[t][:], y_ps[t][:], ACT.Copy, scale=gm_t[:, t : t + 1])
+            nc.scalar.copy(ym[t][:, S:], zero[:].to_broadcast([P, S]))
+        for bank, t, cols in y_banks:
+            nc.scalar.activation(ym[t][:, cols], bank[:], ACT.Copy, scale=gm_t[:, t : t + 1])
+        for bank, t, cols in y_banks:
+            nc.scalar.copy(y[t][:, cols], bank[:])
+        own = new([P, PACK, S], BF16, "own")
         for t in range(PACK):
-            nc.scalar.copy(y[t][:], y_ps[t][:])
-        yn = [sb.tile([P, S], F32, name="yn%d" % t, tag="yn%d" % t, align_bytes=64) for t in range(PACK)]
+            nc.gpsimd.tensor_scalar(own[:, t, :], ym[t][:, :S], 1.0, 0.0, ALU.mult, ALU.add)
         for t in range(PACK):
-            nc.gpsimd.tensor_scalar(ymb[:, t, :], ym[t][:], 1.0, 0.0, ALU.mult, ALU.add)
-        for t in range(PACK):
-            nc.gpsimd.tensor_scalar(yn[t][:], y[t][:], neg_gn[:, t : t + 1], 0.0, ALU.mult, ALU.add)
-        for t in range(PACK):
-            nc.scalar.activation(ex[:, t, :], y_ps[t][:], ACT.Exp)
+            nc.gpsimd.tensor_scalar(yn_ex[t][:, :S], y[t][:], gn_t[:, t : t + 1], 0.0, ALU.mult, ALU.add)
+        for bank, t, cols in y_banks:
+            nc.scalar.activation(yn_ex[t][:, S:][:, cols], bank[:], ACT.Exp)
         ex1 = [new([P, PACK, HALF], F32, "ex1_%d" % a) for a in range(2)]
         for a, (c0, w) in enumerate(HALVES):
             for t in range(PACK):
-                nc.scalar.activation(ex1[a][:, t, :], y[t][:].indirect(entries(l1, c0, w)), ACT.Exp)
+                nc.scalar.activation(ex1[a][:, t, :], y[t][:].indirect(entries(list1, c0, w)), ACT.Exp)
 
-        pa = [new([P, PACK, HALF], BF16, "pa%d" % a) for a in range(2)]
-        pb = [new([P, PACK, HALF], BF16, "pb%d" % a) for a in range(2)]
+        pa = new([P, PACK, S], BF16, "pa")
+        pb = new([P, PACK, S], BF16, "pb")
         for t in range(PACK):
-            for a, (c0, w) in enumerate(HALVES):
-                nc.vector.tensor_copy(pa[a][:, t, :], ym[t][:].indirect(entries(l3, c0, w)))
-                nc.vector.tensor_copy(pb[a][:, t, :], ym[t][:].indirect(entries(l4, c0, w)))
-        w3s = deal_scales(w3s_raw, "w3s")
-        w2s = deal_scales(w2s_raw, "w2s")
-        y2 = [new([P, PACK, HALF], F32, "y2_%d" % a) for a in range(2)]
+            nc.vector.tensor_copy(pa[:, t, :], ym[t][:].indirect(list3[:]))
+            nc.vector.tensor_copy(pb[:, t, :], ym[t][:].indirect(list4[:]))
+        w3_s = new([P, C], U8, "w3_s")
+        w2_s = new([P, C], U8, "w2_s")
+        nc.gpsimd.tensor_copy(dealt_bytes(w3_s), raw_bytes(w3_s_raw))
+        nc.gpsimd.tensor_copy(dealt_bytes(w2_s), raw_bytes(w2_s_raw))
+        yn2 = new([P, PACK, S], F32, "yn2")
         for t in range(PACK):
-            for a, (c0, w) in enumerate(HALVES):
-                nc.vector.tensor_copy(y2[a][:, t, :], yn[t][:].indirect(entries(l2, c0, w)))
-        hi = [sb.tile([P, PACK, HALF], BF16, name="hi0", tag="yn3", align_bytes=64), None]
-        lo = [sb.tile([P, PACK, HALF], BF16, name="lo0", tag="yn2", align_bytes=64), None]
-        mid = [new([P, PACK, HALF], BF16, "mid%d" % a) for a in range(2)]
-        med = new([P, PACK, HALF], BF16, "med")
-
-        def median_bounds(a):
-            c0, w = HALVES[a]
-            nc.vector.tensor_tensor(hi[a][:], ymb[:, :, c0 : c0 + w], pa[a][:], ALU.max)
-            nc.vector.tensor_tensor(lo[a][:], ymb[:, :, c0 : c0 + w], pa[a][:], ALU.min)
-            nc.vector.tensor_tensor(mid[a][:], hi[a][:], pb[a][:], ALU.min)
-
-        median_bounds(0)
-        nc.vector.tensor_tensor(med[:], lo[0][:], mid[0][:], ALU.max)
-
-        sm = [new([P, PACK, HALF], F32, "sm%d" % a) for a in range(2)]
-        lg = [sb.tile([P, PACK, HALF], F32, name="lg%d" % a, tag="lg%d" % a, align_bytes=64) for a in range(2)]
+            nc.vector.tensor_copy(yn2[:, t, :], yn_ex[t][:].indirect(list2[:]))
+        sums = [new([P, PACK, HALF], F32, "sums%d" % a) for a in range(2)]
         for a, (c0, w) in enumerate(HALVES):
-            nc.gpsimd.tensor_tensor(sm[a][:], ex[:, :, c0 : c0 + w], ex1[a][:], ALU.add)
-        for a in range(2):
-            nc.scalar.activation(lg[a][:], sm[a][:], ACT.Ln)
-        lgn = [sb.tile([P, PACK, HALF], F32, name="lgn%d" % a, tag="lgn%d" % a, align_bytes=64) for a in range(2)]
-        for a in range(2):
             for t in range(PACK):
-                nc.scalar.activation(lgn[a][:, t, :], lg[a][:, t, :], ACT.Copy, scale=gn_t[:, t : t + 1])
+                nc.gpsimd.tensor_tensor(sums[a][:, t, :], yn_ex[t][:, S + c0 : S + c0 + w], ex1[a][:, t, :], ALU.add)
 
-        def woven(tile, i):
-            return tile[:].rearrange("p (c i t) -> p c t i", t=PACK, i=i)
+        high0 = new([P, PACK, HALF], BF16, "high0", tag="yn_ex3")
+        low0 = new([P, PACK, HALF], BF16, "low0", tag="yn_ex2")
+        mid = [new([P, PACK, HALF], BF16, "mid%d" % a) for a in range(2)]
+        median0 = new([P, PACK, HALF], BF16, "median0")
+        nc.vector.tensor_tensor(high0[:], own[:, :, :HALF], pa[:, :, :HALF], ALU.max)
+        nc.vector.tensor_tensor(low0[:], own[:, :, :HALF], pa[:, :, :HALF], ALU.min)
+        nc.vector.tensor_tensor(mid[0][:], high0[:], pb[:, :, :HALF], ALU.min)
+        nc.vector.tensor_tensor(median0[:], low0[:], mid[0][:], ALU.max)
 
-        def planar(view, i):
-            return view.rearrange("p t (c i) -> p c t i", i=i)
+        logs = [new([P, PACK, HALF], F32, "logs%d" % a) for a in range(2)]
+        gained = [new([P, PACK, HALF], F32, "gained%d" % a) for a in range(2)]
 
-        z2b = [sb.tile([P, HALF * PACK], BF16, name="z2b%d" % a, tag="lg%d" % (1 - a), align_bytes=64) for a in range(2)]
-        nc.scalar.copy(woven(z2b[0], 4), planar(med[:], 4))
+        def apply_gain(a):
+            for t in range(PACK):
+                nc.scalar.activation(gained[a][:, t, :], logs[a][:, t, :], ACT.Copy, scale=gn_t[:, t : t + 1])
 
-        zb = new([P, S * PACK], BF16, "zb")
-        for a, (c0, w) in enumerate(HALVES):
+        nc.scalar.activation(logs[0][:], sums[0][:], ACT.Ln)
+        apply_gain(0)
+        nc.scalar.activation(logs[1][:], sums[1][:], ACT.Ln)
+        z2_woven = [new([P, HALF * PACK], BF16, "z2_woven%d" % a, tag="sums%d" % (1 - a)) for a in range(2)]
+        nc.scalar.copy(woven(z2_woven[0][:], 4), planar(median0[:], 4))
+        apply_gain(1)
+
+        z_woven = [new([P, w * PACK], BF16, "z_woven%d" % b) for b, (c0, w) in enumerate(BLOCKS)]
+        z_w = new([P, S], U32, "z_w")
+        z_s = new([P, S], U8, "z_s")
+        z2_w = new([P, S], U32, "z2_w")
+        z2_s = new([P, S], U8, "z2_s")
+
+        def quantise(words, scales, block, src):
+            c0, w = block
+            nc.vector.quantize_mx(out=words[:, c0 : c0 + w].bitcast(FP8X4), scales=scales[:, c0 : c0 + w], in_=src[:])
+
+        def weave_z(b):
+            c0, w = BLOCKS[b]
+            a, ca = divmod(c0, HALF)
             nc.vector.tensor_tensor(
-                zb[:, PACK * c0 : PACK * (c0 + w)].rearrange("p (c i t) -> p c t i", t=PACK, i=2),
-                planar(lgn[a][:], 2), planar(y2[a][:], 2), ALU.add)
-        hi[1] = sb.tile([P, PACK, HALF], BF16, name="hi1", tag="lgn1", align_bytes=64)
-        lo[1] = sb.tile([P, PACK, HALF], BF16, name="lo1", tag="lgn0", align_bytes=64)
-        zc = new([P, S], U32, "zc")
-        zs = new([P, S], U8, "zs")
-        z2c = new([P, S], U32, "z2c")
-        z2s = new([P, S], U8, "z2s")
-        nc.vector.quantize_mx(out=z2c[:, 0:HALF].bitcast(FP8X4), scales=z2s[:, 0:HALF], in_=z2b[0][:])
-        nc.vector.quantize_mx(out=zc[:].bitcast(FP8X4), scales=zs[:], in_=zb[:])
-        median_bounds(1)
-        for g in range(0, HALF, GROUP):
-            nc.vector.tensor_tensor(
-                z2b[1][:, PACK * g : PACK * (g + GROUP)].rearrange("p (c i t) -> p c t i", t=PACK, i=4),
-                planar(lo[1][:, :, g : g + GROUP], 4), planar(mid[1][:, :, g : g + GROUP], 4), ALU.max)
-        for g in range(0, HALF, GROUP):
-            cols = slice(HALF + g, HALF + g + GROUP)
-            nc.vector.quantize_mx(out=z2c[:, cols].bitcast(FP8X4), scales=z2s[:, cols], in_=z2b[1][:, PACK * g : PACK * (g + GROUP)])
+                woven(z_woven[b][:], 2),
+                planar(gained[a][:, :, ca : ca + w], 2),
+                planar(yn2[:, :, c0 : c0 + w], 2),
+                ALU.subtract,
+            )
+
+        weave_z(0)
+        quantise(z_w, z_s, BLOCKS[0], z_woven[0])
+        bounds1 = new([P, 2, PACK, HALF], BF16, "bounds1", tag="gained0")
+        high1, low1 = bounds1[:, 0], bounds1[:, 1]
+        nc.vector.tensor_tensor(high1, own[:, :, HALF:], pa[:, :, HALF:], ALU.max)
+        quantise(z2_w, z2_s, HALVES[0], z2_woven[0])
+        nc.vector.tensor_tensor(low1, own[:, :, HALF:], pa[:, :, HALF:], ALU.min)
+        nc.vector.tensor_tensor(mid[1][:], high1, pb[:, :, HALF:], ALU.min)
+        weave_z(1)
+        nc.vector.tensor_tensor(woven(z2_woven[1][:], 4), planar(low1, 4), planar(mid[1][:], 4), ALU.max)
+        quantise(z_w, z_s, BLOCKS[1], z_woven[1])
+        quantise(z2_w, z2_s, HALVES[1], z2_woven[1])
+        weave_z(2)
+        quantise(z_w, z_s, BLOCKS[2], z_woven[2])
 
         h = [new([P, S], F32, "h%d" % t) for t in range(PACK)]
-        sg0 = new([P, S], F32, "sg0")
-
-        def z_pass(bank, t, c):
-            nc.tensor.matmul_mx(out=bank[:, c % HALF : c % HALF + GROUP], rhs=zc[:, c : c + GROUP].bitcast(FP8X4), rhs_scale=zs[:, c : c + GROUP],
-                                start=True, stop=False, **weights(w2w, w2s, t))
-
-        def z2_pass(bank, t, c):
-            nc.tensor.matmul_mx(out=bank[:, c % HALF : c % HALF + GROUP], rhs=z2c[:, c : c + GROUP].bitcast(FP8X4), rhs_scale=z2s[:, c : c + GROUP],
-                                start=False, stop=True, **weights(w3w, w3s, t))
-
-        for a, (c0, w) in enumerate(HALVES):
-            banks = [ps.tile([P, HALF], F32, name="h_ps%d_%d" % (a, t), tag="bank%d" % (PACK * (1 - a) + t)) for t in range(PACK)]
-            for c in range(c0, c0 + w, GROUP):
-                for t in range(PACK):
-                    z_pass(banks[t], t, c)
-                for t in range(PACK):
-                    z2_pass(banks[t], t, c)
-            nc.scalar.activation(sg0[:, c0 : c0 + w], banks[0][:], ACT.Sigmoid)
-            for t in (1, 2, 3, 0) if a == 1 else range(PACK):
-                if a == 0:
-                    nc.scalar.copy(h[t][:, c0 : c0 + w], banks[t][:])
-                else:
+        sigmoid0 = new([P, S], F32, "sigmoid0")
+        with_z = (w2_w, w2_s, z_w, z_s)
+        with_z2 = (w3_w, w3_s, z2_w, z2_s)
+        gathered_first = (1, 2, 3, 0)
+        for b, (c0, w) in enumerate(BLOCKS):
+            first, last = b == 0, b == len(BLOCKS) - 1
+            lowest_bank = PACK * (1 - b % 2)
+            banks = [ps.tile([P, w], F32, name="h_bank%d_%d" % (b, t), tag="bank%d" % (lowest_bank + t)) for t in range(PACK)]
+            for g in range(0, w, GROUP):
+                cols = slice(c0 + g, c0 + g + GROUP)
+                for n, (words, scales, codes, code_scales) in enumerate((with_z2, with_z) if last else (with_z, with_z2)):
+                    for t in range(PACK) if first else gathered_first:
+                        product(banks[t][:, g : g + GROUP], words, scales, t, codes[:, cols], code_scales[:, cols], n == 0, n == 1)
+            if first:
+                nc.scalar.activation(sigmoid0[:, c0 : c0 + w], banks[0][:], ACT.Sigmoid)
+            for t in gathered_first:
+                if last and t in gathered_first[:2]:
                     nc.vector.tensor_copy(h[t][:, c0 : c0 + w], banks[t][:])
+                else:
+                    nc.scalar.copy(h[t][:, c0 : c0 + w], banks[t][:])
+            if not first:
+                nc.scalar.activation(sigmoid0[:, c0 : c0 + w], banks[0][:], ACT.Sigmoid)
 
         out_rows = out_0.rearrange("(p t) c -> p t c", t=PACK)
         out_words = out_1[0].rearrange("p n t -> p (n t)").bitcast(I32)
-        oc = new([P, S], U32, "oc")
-        osc = new([P, S], U8, "osc")
-        o = [new([P, PACK, w], F32, "o%d" % a) for a, (c0, w) in enumerate(Z_BLOCKS)]
-        sg = [new([P, PACK, w], F32, "sg_%d" % a) for a, (c0, w) in enumerate(Z_BLOCKS)]
-        ob = [new([P, w * PACK], BF16, "ob%d" % a) for a, (c0, w) in enumerate(Z_BLOCKS)]
-        for a, (c0, w) in enumerate(Z_BLOCKS):
-            for t in range(1 if a == 0 else 0, PACK):
-                nc.scalar.activation(sg[a][:, t, :], h[t][:].indirect(entries(l5, c0, w)), ACT.Sigmoid)
-        nc.vector.tensor_tensor(o[0][:, 0, :], sg0[:].indirect(entries(l5, 0, HALF)), h[0][:, 0:HALF], ALU.mult)
+        out_w = new([P, S], U32, "out_w")
+        out_s = new([P, S], U8, "out_s")
+        result = [new([P, PACK, HALF], F32, "result%d" % a) for a in range(2)]
+        gate = [new([P, PACK, HALF], F32, "gate%d" % a) for a in range(2)]
+        out_woven = [new([P, w * PACK], BF16, "out_woven%d" % b) for b, (c0, w) in enumerate(BLOCKS)]
+        last_plane = PACK - 1
+        scalar_gathers = [(t, HALVES[0]) for t in range(1, PACK)] + [(t, HALVES[1]) for t in range(1, last_plane)]
+        scalar_gathers = scalar_gathers + [(last_plane, block) for block in BLOCKS[1:]]
+        for t, (c0, w) in scalar_gathers:
+            a, ca = divmod(c0, HALF)
+            nc.scalar.activation(gate[a][:, t, ca : ca + w], h[t][:].indirect(entries(list5, c0, w)), ACT.Sigmoid)
 
-        def planes(a):
-            c0, w = Z_BLOCKS[a]
-            nc.vector.quantize_mx(out=oc[:, c0 : c0 + w].bitcast(FP8X4), scales=osc[:, c0 : c0 + w], in_=ob[a][:])
-            nc.sync.dma_start(out_words[:, c0 : c0 + w], oc[:, c0 : c0 + w].bitcast(I32))
+        def apply_gate(t, block):
+            c0, w = block
+            a, ca = divmod(c0, HALF)
+            factor = sigmoid0[:].indirect(entries(list5, c0, w)) if t == 0 else gate[a][:, t, ca : ca + w]
+            nc.vector.tensor_tensor(result[a][:, t, ca : ca + w], factor, h[t][:, c0 : c0 + w], ALU.mult)
 
-        for a, (c0, w) in enumerate(Z_BLOCKS):
-            for t in range(1 if a == 0 else 0, PACK):
-                nc.vector.tensor_tensor(o[a][:, t, :], sg[a][:, t, :], h[t][:, c0 : c0 + w], ALU.mult)
-            nc.sync.dma_start(out_rows[:, :, c0 : c0 + w], o[a][:])
-            if a > 0:
-                planes(a - 1)
-            nc.vector.tensor_copy(woven(ob[a], 4), planar(o[a][:], 4))
-        planes(len(Z_BLOCKS) - 1)
-        for q in range(4):
-            nc.scalar.dma_start(out_2[0, 4 * q : 4 * q + 4, :].bitcast(I32), osc[32 * q : 32 * q + 4, :].bitcast(I32))
+        def weave_out(b):
+            c0, w = BLOCKS[b]
+            a, ca = divmod(c0, HALF)
+            nc.vector.tensor_copy(woven(out_woven[b][:], 4), planar(result[a][:, :, ca : ca + w], 4))
+
+        def quantise_out(b):
+            c0, w = BLOCKS[b]
+            quantise(out_w, out_s, BLOCKS[b], out_woven[b])
+            nc.sync.dma_start(out_words[:, c0 : c0 + w], out_w[:, c0 : c0 + w].bitcast(I32))
+
+        apply_gate(0, HALVES[0])
+        apply_gate(1, HALVES[0])
+        apply_gate(2, HALVES[0])
+        apply_gate(0, HALVES[1])
+        apply_gate(last_plane, HALVES[0])
+        nc.sync.dma_start(out_rows[:, :, :HALF], result[0][:])
+        weave_out(0)
+        apply_gate(1, HALVES[1])
+        quantise_out(0)
+        apply_gate(2, HALVES[1])
+        nc.sync.dma_start(out_rows[:, :last_plane, HALF:], result[1][:, :last_plane, :])
+        apply_gate(last_plane, BLOCKS[1])
+        weave_out(1)
+        apply_gate(last_plane, BLOCKS[2])
+        nc.sync.dma_start(out_rows[:, last_plane, HALF:], result[1][:, last_plane, :])
+        quantise_out(1)
+        weave_out(2)
+        quantise_out(2)
+        for q in range(P // QUADRANT):
+            queue = nc.scalar if q % 2 == 0 else nc.sync
+            queue.dma_start(out_2[0, PACK * q : PACK * (q + 1), :].bitcast(I32), scale_rows(out_s, q))

@@ -270,7 +270,7 @@ def tile_picked_joinlsemedgate_none_po_kernel(
         out_s = new([P, S], U8, "out_s")
         result = [new([P, PACK, HALF], F32, "result%d" % a) for a in range(2)]
         gate = [new([P, PACK, HALF], F32, "gate%d" % a) for a in range(2)]
-        out_woven = [new([P, w * PACK], BF16, "out_woven%d" % b) for b, (c0, w) in enumerate(BLOCKS)]
+        out_woven = [new([P, HALF * PACK], BF16, "out_woven%d" % a) for a in range(2)]
         last_plane = PACK - 1
         scalar_gathers = [(t, HALVES[0]) for t in range(1, PACK)] + [(t, HALVES[1]) for t in range(1, last_plane)]
         scalar_gathers = scalar_gathers + [(last_plane, block) for block in BLOCKS[1:]]
@@ -284,14 +284,14 @@ def tile_picked_joinlsemedgate_none_po_kernel(
             factor = sigmoid0[:].indirect(entries(list5, c0, w)) if t == 0 else gate[a][:, t, ca : ca + w]
             nc.vector.tensor_tensor(result[a][:, t, ca : ca + w], factor, h[t][:, c0 : c0 + w], ALU.mult)
 
-        def weave_out(b):
+        def weave_out(copy, b):
             c0, w = BLOCKS[b]
             a, ca = divmod(c0, HALF)
-            nc.vector.tensor_copy(woven(out_woven[b][:], 4), planar(result[a][:, :, ca : ca + w], 4))
+            copy(woven(out_woven[a][:, PACK * ca : PACK * (ca + w)], 4), planar(result[a][:, :, ca : ca + w], 4))
 
-        def quantise_out(b):
-            c0, w = BLOCKS[b]
-            quantise(out_w, out_s, BLOCKS[b], out_woven[b])
+        def quantise_out(a):
+            c0, w = HALVES[a]
+            quantise(out_w, out_s, HALVES[a], out_woven[a])
             nc.sync.dma_start(out_words[:, c0 : c0 + w], out_w[:, c0 : c0 + w].bitcast(I32))
 
         apply_gate(0, HALVES[0])
@@ -300,18 +300,17 @@ def tile_picked_joinlsemedgate_none_po_kernel(
         apply_gate(0, HALVES[1])
         apply_gate(last_plane, HALVES[0])
         nc.sync.dma_start(out_rows[:, :, :HALF], result[0][:])
-        weave_out(0)
+        weave_out(nc.vector.tensor_copy, 0)
         apply_gate(1, HALVES[1])
         quantise_out(0)
         apply_gate(2, HALVES[1])
         nc.sync.dma_start(out_rows[:, :last_plane, HALF:], result[1][:, :last_plane, :])
         apply_gate(last_plane, BLOCKS[1])
-        weave_out(1)
+        weave_out(nc.scalar.copy, 1)
         apply_gate(last_plane, BLOCKS[2])
         nc.sync.dma_start(out_rows[:, last_plane, HALF:], result[1][:, last_plane, :])
+        weave_out(nc.vector.tensor_copy, 2)
         quantise_out(1)
-        weave_out(2)
-        quantise_out(2)
         for q in range(P // QUADRANT):
             queue = nc.scalar if q % 2 == 0 else nc.sync
             queue.dma_start(out_2[0, PACK * q : PACK * (q + 1), :].bitcast(I32), scale_rows(out_s, q))

from contextlib import ExitStack

import concourse.mybir as mybir

T = 2048
S = 512
C = 512
FLOPS = 3 * 2 * 512 * C * S

F32 = mybir.dt.float32
BF16 = mybir.dt.bfloat16
I32 = mybir.dt.int32
U32 = mybir.dt.uint32
U16 = mybir.dt.uint16
U8 = mybir.dt.uint8
FP8X4 = mybir.dt.float8_e4m3fn_x4
FP4X4 = mybir.dt.float4_e2m1fn_x4
ALU = mybir.AluOpType
ACT = mybir.ActivationFunctionType

P = 128
PACK = 4
BANKS = 8
LIST_ROWS = 16
QUADRANT = 32
HALF = S // 2
GROUP = 128
HALVES = [(0, HALF), (HALF, HALF)]
BLOCKS = [(0, HALF), (HALF, GROUP), (HALF + GROUP, GROUP)]


def tile_picked_joinlsemedgate_none_po_kernel(
    tc, x_words, x_scales, w1_words, w1_scales, gn, gm, w2_words, w2_scales, w3_words, w3_scales,
    offs, n1, n2, n3, n4, n5, out_0, out_1, out_2,
):
    nc = tc.nc
    with ExitStack() as ctx:
        sb = ctx.enter_context(tc.tile_pool(name="sb", bufs=1))
        ps = ctx.enter_context(tc.psum_pool(name="ps", bufs=1))

        def new(shape, dtype, name, tag=None):
            return sb.tile(shape, dtype, name=name, tag=tag or name, align_bytes=64)

        def load_list(src, name):
            tile = sb.tile([P, S // LIST_ROWS], U16, name=name)
            nc.sync.dma_start(tile[:], src)
            return tile

        def entries(lst, c0, w):
            return lst[:, c0 // LIST_ROWS : (c0 + w) // LIST_ROWS]

        def scale_rows(tile, q):
            return tile[QUADRANT * q : QUADRANT * q + PACK, :].bitcast(I32)

        def load_scales(tile, src):
            for q in range(P // QUADRANT):
                nc.sync.dma_start(scale_rows(tile, q), src[0, PACK * q : PACK * (q + 1), :].bitcast(I32))

        def load_words(src, name):
            raw = new([P, 2 * C], U8, name)
            nc.sync.dma_start(raw[:].bitcast(I32), src[0].bitcast(I32))
            return raw

        def load_gain(queue, tile, src):
            queue.dma_start(tile[:], src.rearrange("(p t) o -> p (t o)", t=PACK))

        def deal_words(raw, name):
            words = new([P, 2 * C], U8, name)
            nc.vector.tensor_copy(
                words[:].rearrange("p (t c i b) -> p c t i b", t=PACK, i=8, b=2),
                raw[:].rearrange("p (c i t b) -> p c t i b", t=PACK, i=8, b=2),
            )
            return words

        def dealt_bytes(tile):
            return tile[:].rearrange("p (t c i) -> p c t i", t=PACK, i=16)

        def raw_bytes(tile):
            return tile[:].rearrange("p (c i t) -> p c t i", t=PACK, i=16)

        def woven(view, run):
            return view.rearrange("p (c i t) -> p c t i", t=PACK, i=run)

        def planar(view, run):
            return view.rearrange("p t (c i) -> p c t i", i=run)

        x_w = new([P, T], I32, "x_w")
        x_s = new([P, T], U8, "x_s")
        w1_s_raw = new([P, C], U8, "w1_s_raw")
        w2_s_raw = new([P, C], U8, "w2_s_raw")
        w3_s_raw = new([P, C], U8, "w3_s_raw")
        gm_t = new([P, PACK], F32, "gm_t")
        gn_t = new([P, PACK], F32, "gn_t")
        nc.gpsimd.memset(x_s[:].bitcast(I32), 0)
        for raw in (w1_s_raw, w3_s_raw, w2_s_raw):
            nc.vector.memset(raw[:].bitcast(I32), 0)

        picks = load_list(offs, "picks")
        w1_w_raw = load_words(w1_words, "w1_w_raw")
        w3_w_raw = load_words(w3_words, "w3_w_raw")
        load_scales(x_s, x_scales)
        nc.sync.dma_start(x_w[:], x_words[0].rearrange("p n t -> p (n t)").bitcast(I32))
        load_gain(nc.gpsimd, gm_t, gm)
        load_scales(w1_s_raw, w1_scales)
        w2_w_raw = load_words(w2_words, "w2_w_raw")
        load_gain(nc.sync, gn_t, gn)
        list3 = load_list(n3, "list3")
        list4 = load_list(n4, "list4")
        list1 = load_list(n1, "list1")
        load_scales(w3_s_raw, w3_scales)
        load_scales(w2_s_raw, w2_scales)
        list2 = load_list(n2, "list2")
        list5 = load_list(n5, "list5")

        w1_w = deal_words(w1_w_raw, "w1_w")
        picked_s = new([P, S], U8, "picked_s")
        picked_w = new([P, S], U32, "picked_w")
        nc.vector.tensor_copy(picked_s[:], x_s[:].indirect(picks[:]))
        w3_w = deal_words(w3_w_raw, "w3_w")
        w1_s = new([P, C], U8, "w1_s")
        nc.vector.tensor_copy(w1_s[:, :P], w1_s_raw[:, ::PACK])
        nc.vector.tensor_copy(dealt_bytes(w1_s)[:, :, 1:, :], raw_bytes(w1_s_raw)[:, :, 1:, :])
        for c0, w in HALVES:
            nc.vector.tensor_copy(picked_w[:, c0 : c0 + w], x_w[:].bitcast(U32).indirect(entries(picks, c0, w)))
        w2_w = deal_words(w2_w_raw, "w2_w")

        def product(bank, words, scales, t, codes, code_scales, start, stop):
            nc.tensor.matmul_mx(
                out=bank,
                lhsT=words[:, 2 * P * t : 2 * P * (t + 1)].bitcast(FP4X4),
                lhsT_scale=scales[:, P * t : P * (t + 1)],
                rhs=codes.bitcast(FP8X4),
                rhs_scale=code_scales,
                start=start,
                stop=stop,
            )

        pieces = [(0, c0, w) for c0, w in HALVES] + [(t, 0, S) for t in range(1, PACK)]
        y_banks = []
        for n, (t, c0, w) in enumerate(pieces):
            bank = ps.tile([P, w], F32, name="y_bank%d" % n, tag="bank%d" % ((n - 1) % BANKS))
            product(bank[:], w1_w, w1_s, t, picked_w[:, c0 : c0 + w], picked_s[:, c0 : c0 + w], True, True)
            y_banks.append((bank, t, slice(c0, c0 + w)))

        ym = [new([P, 2 * S], F32, "ym%d" % t) for t in range(PACK)]
        yn_ex = [new([P, 2 * S], F32, "yn_ex%d" % t) for t in range(PACK)]
        y = [new([P, S], F32, "y%d" % t) for t in range(PACK)]
        zero = new([P, 1], F32, "zero")
        nc.vector.memset(zero[:], 0.0)
        for t in range(PACK):
            nc.scalar.copy(ym[t][:, S:], zero[:].to_broadcast([P, S]))
        for bank, t, cols in y_banks:
            nc.scalar.activation(ym[t][:, cols], bank[:], ACT.Copy, scale=gm_t[:, t : t + 1])
        for bank, t, cols in y_banks:
            nc.scalar.copy(y[t][:, cols], bank[:])
        own = new([P, PACK, S], BF16, "own")
        for t in range(PACK):
            nc.gpsimd.tensor_scalar(own[:, t, :], ym[t][:, :S], 1.0, 0.0, ALU.mult, ALU.add)
        for t in range(PACK):
            nc.gpsimd.tensor_scalar(yn_ex[t][:, :S], y[t][:], gn_t[:, t : t + 1], 0.0, ALU.mult, ALU.add)
        for bank, t, cols in y_banks:
            nc.scalar.activation(yn_ex[t][:, S:][:, cols], bank[:], ACT.Exp)
        ex1 = [new([P, PACK, HALF], F32, "ex1_%d" % a) for a in range(2)]
        for a, (c0, w) in enumerate(HALVES):
            for t in range(PACK):
                nc.scalar.activation(ex1[a][:, t, :], y[t][:].indirect(entries(list1, c0, w)), ACT.Exp)

        pa = new([P, PACK, S], BF16, "pa")
        pb = new([P, PACK, S], BF16, "pb")
        for t in range(PACK):
            nc.vector.tensor_copy(pa[:, t, :], ym[t][:].indirect(list3[:]))
            nc.vector.tensor_copy(pb[:, t, :], ym[t][:].indirect(list4[:]))
        w3_s = new([P, C], U8, "w3_s")
        w2_s = new([P, C], U8, "w2_s")
        nc.gpsimd.tensor_copy(dealt_bytes(w3_s), raw_bytes(w3_s_raw))
        nc.gpsimd.tensor_copy(dealt_bytes(w2_s), raw_bytes(w2_s_raw))
        yn2 = new([P, PACK, S], F32, "yn2")
        for t in range(PACK):
            nc.vector.tensor_copy(yn2[:, t, :], yn_ex[t][:].indirect(list2[:]))
        sums = [new([P, PACK, HALF], F32, "sums%d" % a) for a in range(2)]
        for a, (c0, w) in enumerate(HALVES):
            for t in range(PACK):
                nc.gpsimd.tensor_tensor(sums[a][:, t, :], yn_ex[t][:, S + c0 : S + c0 + w], ex1[a][:, t, :], ALU.add)

        high0 = new([P, PACK, HALF], BF16, "high0", tag="yn_ex3")
        low0 = new([P, PACK, HALF], BF16, "low0", tag="yn_ex2")
        mid = [new([P, PACK, HALF], BF16, "mid%d" % a) for a in range(2)]
        median0 = new([P, PACK, HALF], BF16, "median0")
        nc.vector.tensor_tensor(high0[:], own[:, :, :HALF], pa[:, :, :HALF], ALU.max)
        nc.vector.tensor_tensor(low0[:], own[:, :, :HALF], pa[:, :, :HALF], ALU.min)
        nc.vector.tensor_tensor(mid[0][:], high0[:], pb[:, :, :HALF], ALU.min)
        nc.vector.tensor_tensor(median0[:], low0[:], mid[0][:], ALU.max)

        logs = [new([P, PACK, HALF], F32, "logs%d" % a) for a in range(2)]
        gained = [new([P, PACK, HALF], F32, "gained%d" % a) for a in range(2)]

        def apply_gain(a):
            for t in range(PACK):
                nc.scalar.activation(gained[a][:, t, :], logs[a][:, t, :], ACT.Copy, scale=gn_t[:, t : t + 1])

        nc.scalar.activation(logs[0][:], sums[0][:], ACT.Ln)
        apply_gain(0)
        nc.scalar.activation(logs[1][:], sums[1][:], ACT.Ln)
        z2_woven = [new([P, HALF * PACK], BF16, "z2_woven%d" % a, tag="sums%d" % (1 - a)) for a in range(2)]
        nc.scalar.copy(woven(z2_woven[0][:], 4), planar(median0[:], 4))
        apply_gain(1)

        z_woven = [new([P, w * PACK], BF16, "z_woven%d" % b) for b, (c0, w) in enumerate(BLOCKS)]
        z_w = new([P, S], U32, "z_w")
        z_s = new([P, S], U8, "z_s")
        z2_w = new([P, S], U32, "z2_w")
        z2_s = new([P, S], U8, "z2_s")

        def quantise(words, scales, block, src):
            c0, w = block
            nc.vector.quantize_mx(out=words[:, c0 : c0 + w].bitcast(FP8X4), scales=scales[:, c0 : c0 + w], in_=src[:])

        def weave_z(b):
            c0, w = BLOCKS[b]
            a, ca = divmod(c0, HALF)
            nc.vector.tensor_tensor(
                woven(z_woven[b][:], 2),
                planar(gained[a][:, :, ca : ca + w], 2),
                planar(yn2[:, :, c0 : c0 + w], 2),
                ALU.subtract,
            )

        weave_z(0)
        quantise(z_w, z_s, BLOCKS[0], z_woven[0])
        bounds1 = new([P, 2, PACK, HALF], BF16, "bounds1", tag="gained0")
        high1, low1 = bounds1[:, 0], bounds1[:, 1]
        nc.vector.tensor_tensor(high1, own[:, :, HALF:], pa[:, :, HALF:], ALU.max)
        quantise(z2_w, z2_s, HALVES[0], z2_woven[0])
        nc.vector.tensor_tensor(low1, own[:, :, HALF:], pa[:, :, HALF:], ALU.min)
        nc.vector.tensor_tensor(mid[1][:], high1, pb[:, :, HALF:], ALU.min)
        weave_z(1)
        nc.vector.tensor_tensor(woven(z2_woven[1][:], 4), planar(low1, 4), planar(mid[1][:], 4), ALU.max)
        quantise(z_w, z_s, BLOCKS[1], z_woven[1])
        quantise(z2_w, z2_s, HALVES[1], z2_woven[1])
        weave_z(2)
        quantise(z_w, z_s, BLOCKS[2], z_woven[2])

        h = [new([P, S], F32, "h%d" % t) for t in range(PACK)]
        sigmoid0 = new([P, S], F32, "sigmoid0")
        with_z = (w2_w, w2_s, z_w, z_s)
        with_z2 = (w3_w, w3_s, z2_w, z2_s)
        gathered_first = (1, 2, 3, 0)
        for b, (c0, w) in enumerate(BLOCKS):
            first, last = b == 0, b == len(BLOCKS) - 1
            lowest_bank = PACK * (1 - b % 2)
            banks = [ps.tile([P, w], F32, name="h_bank%d_%d" % (b, t), tag="bank%d" % (lowest_bank + t)) for t in range(PACK)]
            for g in range(0, w, GROUP):
                cols = slice(c0 + g, c0 + g + GROUP)
                for n, (words, scales, codes, code_scales) in enumerate((with_z2, with_z) if last else (with_z, with_z2)):
                    for t in range(PACK) if first else gathered_first:
                        product(banks[t][:, g : g + GROUP], words, scales, t, codes[:, cols], code_scales[:, cols], n == 0, n == 1)
            if first:
                nc.scalar.activation(sigmoid0[:, c0 : c0 + w], banks[0][:], ACT.Sigmoid)
            for t in gathered_first:
                if last and t in gathered_first[:2]:
                    nc.vector.tensor_copy(h[t][:, c0 : c0 + w], banks[t][:])
                else:
                    nc.scalar.copy(h[t][:, c0 : c0 + w], banks[t][:])
            if not first:
                nc.scalar.activation(sigmoid0[:, c0 : c0 + w], banks[0][:], ACT.Sigmoid)

        out_rows = out_0.rearrange("(p t) c -> p t c", t=PACK)
        out_words = out_1[0].rearrange("p n t -> p (n t)").bitcast(I32)
        out_w = new([P, S], U32, "out_w")
        out_s = new([P, S], U8, "out_s")
        result = [new([P, PACK, HALF], F32, "result%d" % a) for a in range(2)]
        gate = [new([P, PACK, HALF], F32, "gate%d" % a) for a in range(2)]
        out_woven = [new([P, HALF * PACK], BF16, "out_woven%d" % a) for a in range(2)]
        last_plane = PACK - 1
        scalar_gathers = [(t, HALVES[0]) for t in range(1, PACK)] + [(t, HALVES[1]) for t in range(1, last_plane)]
        scalar_gathers = scalar_gathers + [(last_plane, block) for block in BLOCKS[1:]]
        for t, (c0, w) in scalar_gathers:
            a, ca = divmod(c0, HALF)
            nc.scalar.activation(gate[a][:, t, ca : ca + w], h[t][:].indirect(entries(list5, c0, w)), ACT.Sigmoid)

        def apply_gate(t, block):
            c0, w = block
            a, ca = divmod(c0, HALF)
            factor = sigmoid0[:].indirect(entries(list5, c0, w)) if t == 0 else gate[a][:, t, ca : ca + w]
            nc.vector.tensor_tensor(result[a][:, t, ca : ca + w], factor, h[t][:, c0 : c0 + w], ALU.mult)

        def weave_out(copy, b):
            c0, w = BLOCKS[b]
            a, ca = divmod(c0, HALF)
            copy(woven(out_woven[a][:, PACK * ca : PACK * (ca + w)], 4), planar(result[a][:, :, ca : ca + w], 4))

        def quantise_out(a):
            c0, w = HALVES[a]
            quantise(out_w, out_s, HALVES[a], out_woven[a])
            nc.sync.dma_start(out_words[:, c0 : c0 + w], out_w[:, c0 : c0 + w].bitcast(I32))

        apply_gate(0, HALVES[0])
        apply_gate(1, HALVES[0])
        apply_gate(2, HALVES[0])
        apply_gate(0, HALVES[1])
        apply_gate(last_plane, HALVES[0])
        nc.sync.dma_start(out_rows[:, :, :HALF], result[0][:])
        weave_out(nc.vector.tensor_copy, 0)
        apply_gate(1, HALVES[1])
        quantise_out(0)
        apply_gate(2, HALVES[1])
        nc.sync.dma_start(out_rows[:, :last_plane, HALF:], result[1][:, :last_plane, :])
        apply_gate(last_plane, BLOCKS[1])
        weave_out(nc.scalar.copy, 1)
        apply_gate(last_plane, BLOCKS[2])
        nc.sync.dma_start(out_rows[:, last_plane, HALF:], result[1][:, last_plane, :])
        weave_out(nc.vector.tensor_copy, 2)
        quantise_out(1)
        for q in range(P // QUADRANT):
            queue = nc.scalar if q % 2 == 0 else nc.sync
            queue.dma_start(out_2[0, PACK * q : PACK * (q + 1), :].bitcast(I32), scale_rows(out_s, q))
